import numpy as np
CORES = [3,0,2,1,6,7,4,5]
N = 8
def setup_inputs(rng):
    return {"x": rng.standard_normal((N, 128, 8), dtype=np.float32)}
def reference(x):
    b = 8 // N
    blocks = x.reshape(N, 128, N, b)
    return {"y": np.ascontiguousarray(blocks.transpose(2, 1, 0, 3)).reshape(N, 128, 8)}

from concourse.bass import DstId, RemoteDMATransfer

SCRATCH = {
    "send": ("sbuf", [128, 8], "float32"),
    "land": ("sbuf", [128, 8], "float32"),
}
SEMAPHORES = ["loaded", "read", "arrived", "stored"]

ENGINES = 2


def rank_program(g, core, T, topo):
    rank = T.rank_of(core)
    if rank is None:
        return
    n = len(T.cores)

    g.dma_start(T.send[:], T.x[:]).then_inc(T.sem.loaded, 16)
    g.wait_ge(T.sem.loaded, 16)

    transfers = []
    for k, j in enumerate([j for j in range(n) if j != rank]):
        rid, pid, sengine = topo.addr(T.cores[j])
        transfers.append(RemoteDMATransfer(
            dst_ids=[DstId(rid=rid, pnc=pid)],
            dma_engine_mask=((1 << ENGINES) - 1) << (ENGINES * k),
            remote_sem=T.sem.arrived,
            src=T.send[:, j:j + 1],
            dst=T.land[:, rank:rank + 1],
        ))
    g.remote_dma_fused(transfers, local_sem=T.sem.read)

    g.dma_start(T.land[:, rank:rank + 1], T.send[:, rank:rank + 1]).then_inc(T.sem.loaded, 16)

    g.wait_ge(T.sem.loaded, 32)
    g.wait_ge(T.sem.arrived, ENGINES * (n - 1))
    g.dma_start(T.y[:], T.land[:]).then_inc(T.sem.stored, 16)
    g.wait_ge(T.sem.read, ENGINES * (n - 1))
    g.wait_ge(T.sem.stored, 16)
